import numpy as np, ml_dtypes
CORES = [10,34,74,98]
N = 4
import mx_ref
NC = 512
BF = ml_dtypes.bfloat16
def setup_inputs(rng):
    def f(*shape):
        return mx_ref.flush((rng.standard_normal(shape, dtype=np.float32) * np.exp2(rng.integers(-2, 3, shape[:-1] + (1,)))).astype(BF))
    return {"c": f(N, 128, 512), "x": f(N, 128, 4 * NC)}
def setup_inputs_blocks(rng):
    d = setup_inputs(rng)
    for k in ("c", "x"): d[k] = mx_ref.spread(d[k], rng, 1)
    return d
def setup_inputs_wide(rng):
    d = setup_inputs(rng)
    for k in ("c", "x"): d[k] = mx_ref.flush((d[k].astype(np.float32) * np.exp2(rng.integers(-8, 9, (N, 1, 1))).astype(np.float32)).astype(BF))
    return d
def setup_inputs_zeros(rng):
    d = setup_inputs(rng); v = d["x"].reshape(N, 128, -1, 4).copy()
    v[np.broadcast_to((rng.random((N, 1, v.shape[2], 1)) < 0.33), v.shape)] = 0
    d["x"] = v.reshape(d["x"].shape)
    return d
def reference(c, x):
    QC = [mx_ref.quantize(c[k]) for k in range(N)]; QX = [mx_ref.quantize(x[j]) for j in range(N)]
    y = np.zeros((N, 128, NC), np.float32)
    for r in range(N):
        for j in range(N):
            p = mx_ref.matmul(QC[(r - j) % N], QX[j])
            y[r] = p if j == 0 else y[r] + p
    return {"y": y}

@@ -1,0 +1,220 @@
+from concourse.bass import DstId, RemoteDMATransfer
+from concourse.mybir import dt, ActivationFunctionType
+
+N = 4
+NCORES = 112
+CW = 128
+XW = 512
+CH = 128
+NQ = XW // CH
+W = CW + XW
+
+PIECES = {
+    "ca": ("Q", 0, 64, 0),
+    "cb": ("Q", 64, 128, 1),
+    "cs": ("S", 0, 128, 2),
+    "x0": ("Q", 128, 256, 0),
+    "x1": ("Q", 256, 384, 1),
+    "x2": ("Q", 384, 512, 2),
+    "xs": ("S", 128, 640, -1),
+    "x3": ("Q", 512, 640, -1),
+}
+STEPS = [("ca", "cb"), ("cs",), ("x0",), ("x1",), ("x2",), ("xs",), ("x3",)]
+LOADS = [(0, 384), (384, 512)]
+WAVES = [0, 1, 2, 3]
+
+SCRATCH = {
+    "cbf": ("sbuf", [128, 4 * CW], "bfloat16"),
+    "xbf": ("sbuf", [128, 4 * XW], "bfloat16"),
+    "acc": ("psum", [128, 512 * NQ], "float32"),
+    "yb": ("sbuf", [128, XW], "float32"),
+}
+for _s in range(N):
+    SCRATCH["Q%d" % _s] = ("sbuf", [128, W], "float8_e4m3fn_x4")
+    SCRATCH["S%d" % _s] = ("sbuf", [128, W], "uint8")
+
+SEMAPHORES = (["ldc", "sent"] + ["ldx%d" % i for i in range(len(LOADS))] + ["qz%d" % i for i in range(NQ + 1)]
+              + ["mm%d" % q for q in range(NQ)] + ["cp%d" % q for q in range(NQ)] + ["st%d" % q for q in range(NQ)]
+              + ["f_%s" % p for p in PIECES] + ["a%d_%s" % (s, p) for s in range(N) for p in PIECES])
+
+
+def _bits(m):
+    return [b for b in range(m.bit_length()) if (m >> b) & 1]
+
+
+def _helpers(T, topo, s):
+    home = T.cores[s]
+    others = [c for c in T.cores if c != home]
+    hs = [c for c in range(NCORES)
+          if c not in T.cores and topo.chip(c) == topo.chip(home) and all(topo.may_write(c, d) for d in others)]
+    hs.sort(key=lambda c: (topo.die(c) == topo.die(home), c))
+    return hs
+
+
+def _view(T, s, name):
+    kind, lo, hi, _c = PIECES[name]
+    if kind == "Q":
+        return T["Q%d" % s][:, lo:hi].bitcast(dt.uint8)
+    return T["S%d" % s][:, lo:hi]
+
+
+def _fan_mask(T, topo, core, s):
+    m = None
+    for d in T.cores:
+        if d != T.cores[s]:
+            m = topo.mask(core, d) if m is None else (m & topo.mask(core, d))
+    return m
+
+
+def _fan(g, core, s, name, T, topo):
+    dests = [c for c in T.cores if c != T.cores[s]]
+    m = _fan_mask(T, topo, core, s)
+    ids = []
+    for d in dests:
+        rid, pid, _se = topo.addr(d)
+        ids.append(DstId(rid=rid, pnc=pid))
+    g.remote_dma_fused(
+        [RemoteDMATransfer(dst_ids=ids, dma_engine_mask=m, remote_sem=T.sem["a%d_%s" % (s, name)],
+                           srcs=[_view(T, s, name)], dsts=[_view(T, s, name) for _d in dests])],
+        local_sem=T.sem.sent)
+    return len(_bits(m))
+
+
+def _feed_counts(T, topo, s):
+    home = T.cores[s]
+    hs = _helpers(T, topo, s)
+    out = {}
+    for step in STEPS:
+        if PIECES[step[0]][3] < 0:
+            continue
+        parts = 1
+        while parts < len(step):
+            parts *= 2
+        for i, name in enumerate(step):
+            h = hs[PIECES[name][3]]
+            bits = _bits(topo.mask(home, h))
+            per = len(bits) // parts
+            out[name] = (h, sum(1 << b for b in bits[i * per:(i + 1) * per]))
+    return out
+
+
+def _chunks_of(lo, hi):
+    return [i for i in range(NQ + 1) if lo < (i + 1) * CH and hi > i * CH]
+
+
+def _helper(g, core, s, idx, T, topo):
+    feeds = _feed_counts(T, topo, s)
+    sent = 0
+    for step in STEPS:
+        for name in step:
+            if PIECES[name][3] == idx:
+                g.wait_ge(T.sem["f_%s" % name], len(_bits(feeds[name][1])))
+                sent += _fan(g, core, s, name, T, topo)
+    g.wait_ge(T.sem.sent, sent)
+
+
+def _rank(g, core, r, T, topo):
+    Q, S = T["Q%d" % r], T["S%d" % r]
+    g.sync.dma_start(T.cbf[:], T.c[:]).then_inc(T.sem.ldc, 16)
+    for i, (lo, hi) in enumerate(LOADS):
+        g.sync.dma_start(T.xbf[:, 4 * lo:4 * hi], T.x[:, 4 * lo:4 * hi]).then_inc(T.sem["ldx%d" % i], 16)
+    g.vector.wait_ge(T.sem.ldc, 16)
+    g.vector.quantize_mx(Q[:, 0:CW], S[:, 0:CW], T.cbf[:]).then_inc(T.sem.qz0, 1)
+    seen = set()
+    for q in range(NQ):
+        for i, (lo, hi) in enumerate(LOADS):
+            if lo < (q + 1) * CH and hi > q * CH and i not in seen:
+                seen.add(i)
+                g.vector.wait_ge(T.sem["ldx%d" % i], 16)
+        a = CW + q * CH
+        g.vector.quantize_mx(Q[:, a:a + CH], S[:, a:a + CH],
+                             T.xbf[:, 4 * q * CH:4 * (q + 1) * CH]).then_inc(T.sem["qz%d" % (q + 1)], 1)
+    feeds = _feed_counts(T, topo, r)
+    sent = 0
+    ready = set()
+    for step in STEPS:
+        for name in step:
+            for i in _chunks_of(PIECES[name][1], PIECES[name][2]):
+                if i not in ready:
+                    ready.add(i)
+                    g.wait_ge(T.sem["qz%d" % i], 1)
+        if PIECES[step[0]][3] < 0:
+            for name in step:
+                sent += _fan(g, core, r, name, T, topo)
+        elif len(step) == 1:
+            name = step[0]
+            h, m = feeds[name]
+            rid, pid, _se = topo.addr(h)
+            g.remote_dma(out_ap=_view(T, r, name), in_ap=_view(T, r, name), remote_sem=T.sem["f_%s" % name],
+                         local_sem=T.sem.sent, pid=pid, routing_id=rid, dma_engine_mask=m)
+            sent += len(_bits(m))
+        else:
+            trs = []
+            for name in step:
+                h, m = feeds[name]
+                rid, pid, _se = topo.addr(h)
+                trs.append(RemoteDMATransfer(dst_ids=[DstId(rid=rid, pnc=pid)], dma_engine_mask=m,
+                                             remote_sem=T.sem["f_%s" % name], src=_view(T, r, name),
+                                             dst=_view(T, r, name)))
+                sent += len(_bits(m))
+            g.remote_dma_fused(trs, local_sem=T.sem.sent)
+    g.wait_ge(T.sem.sent, sent)
+    hs_of = [_helpers(T, topo, s) for s in range(N)]
+    got = set()
+
+    def need(s, lo, hi):
+        if s == r:
+            for i in _chunks_of(lo, hi):
+                if ("q", i) not in got:
+                    got.add(("q", i))
+                    g.tensor.wait_ge(T.sem["qz%d" % i], 1)
+            return
+        for name, (_k, plo, phi, car) in PIECES.items():
+            if plo < hi and phi > lo and (s, name) not in got:
+                got.add((s, name))
+                sender = T.cores[s] if car < 0 else hs_of[s][car]
+                g.tensor.wait_ge(T.sem["a%d_%s" % (s, name)], len(_bits(_fan_mask(T, topo, sender, s))))
+
+    seq = [(r, q) for q in WAVES] + [((r - d) % N, q) for q in WAVES for d in range(1, N)]
+    done = [0] * NQ
+    for j, q in seq:
+        k = (r - j) % N
+        a = CW + q * CH
+        need(k, 0, CW)
+        need(j, a, a + CH)
+        done[q] += 1
+        mm = g.tensor.matmul_mx(T.acc[:, 512 * q:512 * q + CH], T["Q%d" % k][:, 0:CW], T["S%d" % k][:, 0:CW],
+                                T["Q%d" % j][:, a:a + CH], T["S%d" % j][:, a:a + CH], done[q] == 1, done[q] == N)
+        if done[q] == N:
+            mm.then_inc(T.sem["mm%d" % q], 1)
+    mine = {"scalar": [], "sync": []}
+    for n, q in enumerate(WAVES):
+        ysb, bank, yo = T.yb[:, q * CH:(q + 1) * CH], T.acc[:, 512 * q:512 * q + CH], T.y[:, q * CH:(q + 1) * CH]
+        if (len(WAVES) - 1 - n) % 2:
+            g.scalar.wait_ge(T.sem["mm%d" % q], 1)
+            g.scalar.activation(ysb, bank, ActivationFunctionType.Copy).then_inc(T.sem["cp%d" % q], 1)
+            g.scalar.wait_ge(T.sem["cp%d" % q], 1)
+            g.scalar.dma_start(yo, ysb).then_inc(T.sem["st%d" % q], 16)
+            mine["scalar"].append(q)
+        else:
+            g.vector.wait_ge(T.sem["mm%d" % q], 1)
+            g.vector.tensor_copy(ysb, bank).then_inc(T.sem["cp%d" % q], 1)
+            g.sync.wait_ge(T.sem["cp%d" % q], 1)
+            g.sync.dma_start(yo, ysb).then_inc(T.sem["st%d" % q], 16)
+            mine["sync"].append(q)
+    for q in mine["scalar"]:
+        g.scalar.wait_ge(T.sem["st%d" % q], 16)
+    for q in mine["sync"]:
+        g.sync.wait_ge(T.sem["st%d" % q], 16)
+
+
+def rank_program(g, core, T, topo):
+    rank = T.rank_of(core)
+    if rank is not None:
+        _rank(g, core, rank, T, topo)
+        return
+    for s in range(N):
+        hs = _helpers(T, topo, s)
+        if core in hs:
+            _helper(g, core, s, hs.index(core), T, topo)
+            return

@@ -9,19 +9,20 @@ CH = 128
 NQ = XW // CH
 W = CW + XW
 
+QCH = [(0, 128), (128, 320), (320, 512), (512, 640)]
 PIECES = {
     "ca": ("Q", 0, 64, 0),
     "cb": ("Q", 64, 128, 1),
     "cs": ("S", 0, 128, 2),
-    "x0": ("Q", 128, 256, 0),
-    "x1": ("Q", 256, 384, 1),
-    "x2": ("Q", 384, 512, 2),
+    "x1": ("Q", 128, 224, 0),
+    "x2": ("Q", 224, 320, 1),
+    "xr": ("Q", 320, 512, -1),
+    "x3": ("Q", 512, 640, 2),
     "xs": ("S", 128, 640, -1),
-    "x3": ("Q", 512, 640, -1),
 }
-STEPS = [("ca", "cb"), ("cs",), ("x0",), ("x1",), ("x2",), ("xs",), ("x3",)]
-LOADS = [(0, 384), (384, 512)]
-WAVES = [0, 1, 2, 3]
+STEPS = [("ca", "cb"), ("cs",), ("x1", "x2"), ("xr",), ("x3",), ("xs",)]
+ON_CHIP_ENGINES_ONLY = ("x3",)
+WAVES = [2, 0, 1, 3]
 
 SCRATCH = {
     "cbf": ("sbuf", [128, 4 * CW], "bfloat16"),
@@ -33,7 +34,7 @@ for _s in range(N):
     SCRATCH["Q%d" % _s] = ("sbuf", [128, W], "float8_e4m3fn_x4")
     SCRATCH["S%d" % _s] = ("sbuf", [128, W], "uint8")
 
-SEMAPHORES = (["ldc", "sent"] + ["ldx%d" % i for i in range(len(LOADS))] + ["qz%d" % i for i in range(NQ + 1)]
+SEMAPHORES = (["sent"] + ["ld%d" % i for i in range(len(QCH))] + ["qz%d" % i for i in range(len(QCH))]
               + ["mm%d" % q for q in range(NQ)] + ["cp%d" % q for q in range(NQ)] + ["st%d" % q for q in range(NQ)]
               + ["f_%s" % p for p in PIECES] + ["a%d_%s" % (s, p) for s in range(N) for p in PIECES])
 
@@ -58,16 +59,19 @@ def _view(T, s, name):
     return T["S%d" % s][:, lo:hi]
 
 
+def _dests(T, s):
+    return [T.cores[(s + d) % N] for d in range(1, N)]
+
+
 def _fan_mask(T, topo, core, s):
     m = None
-    for d in T.cores:
-        if d != T.cores[s]:
-            m = topo.mask(core, d) if m is None else (m & topo.mask(core, d))
+    for d in _dests(T, s):
+        m = topo.mask(core, d) if m is None else (m & topo.mask(core, d))
     return m
 
 
 def _fan(g, core, s, name, T, topo):
-    dests = [c for c in T.cores if c != T.cores[s]]
+    dests = _dests(T, s)
     m = _fan_mask(T, topo, core, s)
     ids = []
     for d in dests:
@@ -92,14 +96,17 @@ def _feed_counts(T, topo, s):
             parts *= 2
         for i, name in enumerate(step):
             h = hs[PIECES[name][3]]
-            bits = _bits(topo.mask(home, h))
+            full = topo.mask(home, h)
+            if name in ON_CHIP_ENGINES_ONLY:
+                full = full & ~_fan_mask(T, topo, home, s)
+            bits = _bits(full)
             per = len(bits) // parts
             out[name] = (h, sum(1 << b for b in bits[i * per:(i + 1) * per]))
     return out
 
 
 def _chunks_of(lo, hi):
-    return [i for i in range(NQ + 1) if lo < (i + 1) * CH and hi > i * CH]
+    return [i for i, (a, b) in enumerate(QCH) if lo < b and hi > a]
 
 
 def _helper(g, core, s, idx, T, topo):
@@ -115,20 +122,16 @@ def _helper(g, core, s, idx, T, topo):
 
 def _rank(g, core, r, T, topo):
     Q, S = T["Q%d" % r], T["S%d" % r]
-    g.sync.dma_start(T.cbf[:], T.c[:]).then_inc(T.sem.ldc, 16)
-    for i, (lo, hi) in enumerate(LOADS):
-        g.sync.dma_start(T.xbf[:, 4 * lo:4 * hi], T.x[:, 4 * lo:4 * hi]).then_inc(T.sem["ldx%d" % i], 16)
-    g.vector.wait_ge(T.sem.ldc, 16)
-    g.vector.quantize_mx(Q[:, 0:CW], S[:, 0:CW], T.cbf[:]).then_inc(T.sem.qz0, 1)
-    seen = set()
-    for q in range(NQ):
-        for i, (lo, hi) in enumerate(LOADS):
-            if lo < (q + 1) * CH and hi > q * CH and i not in seen:
-                seen.add(i)
-                g.vector.wait_ge(T.sem["ldx%d" % i], 16)
-        a = CW + q * CH
-        g.vector.quantize_mx(Q[:, a:a + CH], S[:, a:a + CH],
-                             T.xbf[:, 4 * q * CH:4 * (q + 1) * CH]).then_inc(T.sem["qz%d" % (q + 1)], 1)
+    for i, (a, b) in enumerate(QCH):
+        if i == 0:
+            g.sync.dma_start(T.cbf[:], T.c[:]).then_inc(T.sem.ld0, 16)
+        else:
+            lo, hi = 4 * (a - CW), 4 * (b - CW)
+            g.sync.dma_start(T.xbf[:, lo:hi], T.x[:, lo:hi]).then_inc(T.sem["ld%d" % i], 16)
+    for i, (a, b) in enumerate(QCH):
+        g.vector.wait_ge(T.sem["ld%d" % i], 16)
+        tile = T.cbf[:] if i == 0 else T.xbf[:, 4 * (a - CW):4 * (b - CW)]
+        g.vector.quantize_mx(Q[:, a:b], S[:, a:b], tile).then_inc(T.sem["qz%d" % i], 1)
     feeds = _feed_counts(T, topo, r)
     sent = 0
     ready = set()
@@ -175,7 +178,7 @@ def _rank(g, core, r, T, topo):
                 sender = T.cores[s] if car < 0 else hs_of[s][car]
                 g.tensor.wait_ge(T.sem["a%d_%s" % (s, name)], len(_bits(_fan_mask(T, topo, sender, s))))
 
-    seq = [(r, q) for q in WAVES] + [((r - d) % N, q) for q in WAVES for d in range(1, N)]
+    seq = [((r - d) % N, q) for d in range(N) for q in WAVES]
     done = [0] * NQ
     for j, q in seq:
         k = (r - j) % N

from concourse.bass import DstId, RemoteDMATransfer
from concourse.mybir import dt, ActivationFunctionType

N = 4
NCORES = 112
CW = 128
XW = 512
CH = 128
NQ = XW // CH
W = CW + XW

QCH = [(0, 128), (128, 320), (320, 512), (512, 640)]
PIECES = {
    "ca": ("Q", 0, 64, 0),
    "cb": ("Q", 64, 128, 1),
    "cs": ("S", 0, 128, 2),
    "x1": ("Q", 128, 224, 0),
    "x2": ("Q", 224, 320, 1),
    "xr": ("Q", 320, 512, -1),
    "x3": ("Q", 512, 640, 2),
    "xs": ("S", 128, 640, -1),
}
STEPS = [("ca", "cb"), ("cs",), ("x1", "x2"), ("xr",), ("x3",), ("xs",)]
ON_CHIP_ENGINES_ONLY = ("x3",)
WAVES = [2, 0, 1, 3]

SCRATCH = {
    "cbf": ("sbuf", [128, 4 * CW], "bfloat16"),
    "xbf": ("sbuf", [128, 4 * XW], "bfloat16"),
    "acc": ("psum", [128, 512 * NQ], "float32"),
    "yb": ("sbuf", [128, XW], "float32"),
}
for _s in range(N):
    SCRATCH["Q%d" % _s] = ("sbuf", [128, W], "float8_e4m3fn_x4")
    SCRATCH["S%d" % _s] = ("sbuf", [128, W], "uint8")

SEMAPHORES = (["sent"] + ["ld%d" % i for i in range(len(QCH))] + ["qz%d" % i for i in range(len(QCH))]
              + ["mm%d" % q for q in range(NQ)] + ["cp%d" % q for q in range(NQ)] + ["st%d" % q for q in range(NQ)]
              + ["f_%s" % p for p in PIECES] + ["a%d_%s" % (s, p) for s in range(N) for p in PIECES])


def _bits(m):
    return [b for b in range(m.bit_length()) if (m >> b) & 1]


def _helpers(T, topo, s):
    home = T.cores[s]
    others = [c for c in T.cores if c != home]
    hs = [c for c in range(NCORES)
          if c not in T.cores and topo.chip(c) == topo.chip(home) and all(topo.may_write(c, d) for d in others)]
    hs.sort(key=lambda c: (topo.die(c) == topo.die(home), c))
    return hs


def _view(T, s, name):
    kind, lo, hi, _c = PIECES[name]
    if kind == "Q":
        return T["Q%d" % s][:, lo:hi].bitcast(dt.uint8)
    return T["S%d" % s][:, lo:hi]


def _dests(T, s):
    return [T.cores[(s + d) % N] for d in range(1, N)]


def _fan_mask(T, topo, core, s):
    m = None
    for d in _dests(T, s):
        m = topo.mask(core, d) if m is None else (m & topo.mask(core, d))
    return m


def _fan(g, core, s, name, T, topo):
    dests = _dests(T, s)
    m = _fan_mask(T, topo, core, s)
    ids = []
    for d in dests:
        rid, pid, _se = topo.addr(d)
        ids.append(DstId(rid=rid, pnc=pid))
    g.remote_dma_fused(
        [RemoteDMATransfer(dst_ids=ids, dma_engine_mask=m, remote_sem=T.sem["a%d_%s" % (s, name)],
                           srcs=[_view(T, s, name)], dsts=[_view(T, s, name) for _d in dests])],
        local_sem=T.sem.sent)
    return len(_bits(m))


def _feed_counts(T, topo, s):
    home = T.cores[s]
    hs = _helpers(T, topo, s)
    out = {}
    for step in STEPS:
        if PIECES[step[0]][3] < 0:
            continue
        parts = 1
        while parts < len(step):
            parts *= 2
        for i, name in enumerate(step):
            h = hs[PIECES[name][3]]
            full = topo.mask(home, h)
            if name in ON_CHIP_ENGINES_ONLY:
                full = full & ~_fan_mask(T, topo, home, s)
            bits = _bits(full)
            per = len(bits) // parts
            out[name] = (h, sum(1 << b for b in bits[i * per:(i + 1) * per]))
    return out


def _chunks_of(lo, hi):
    return [i for i, (a, b) in enumerate(QCH) if lo < b and hi > a]


def _helper(g, core, s, idx, T, topo):
    feeds = _feed_counts(T, topo, s)
    sent = 0
    for step in STEPS:
        for name in step:
            if PIECES[name][3] == idx:
                g.wait_ge(T.sem["f_%s" % name], len(_bits(feeds[name][1])))
                sent += _fan(g, core, s, name, T, topo)
    g.wait_ge(T.sem.sent, sent)


def _rank(g, core, r, T, topo):
    Q, S = T["Q%d" % r], T["S%d" % r]
    for i, (a, b) in enumerate(QCH):
        if i == 0:
            g.sync.dma_start(T.cbf[:], T.c[:]).then_inc(T.sem.ld0, 16)
        else:
            lo, hi = 4 * (a - CW), 4 * (b - CW)
            g.sync.dma_start(T.xbf[:, lo:hi], T.x[:, lo:hi]).then_inc(T.sem["ld%d" % i], 16)
    for i, (a, b) in enumerate(QCH):
        g.vector.wait_ge(T.sem["ld%d" % i], 16)
        tile = T.cbf[:] if i == 0 else T.xbf[:, 4 * (a - CW):4 * (b - CW)]
        g.vector.quantize_mx(Q[:, a:b], S[:, a:b], tile).then_inc(T.sem["qz%d" % i], 1)
    feeds = _feed_counts(T, topo, r)
    sent = 0
    ready = set()
    for step in STEPS:
        for name in step:
            for i in _chunks_of(PIECES[name][1], PIECES[name][2]):
                if i not in ready:
                    ready.add(i)
                    g.wait_ge(T.sem["qz%d" % i], 1)
        if PIECES[step[0]][3] < 0:
            for name in step:
                sent += _fan(g, core, r, name, T, topo)
        elif len(step) == 1:
            name = step[0]
            h, m = feeds[name]
            rid, pid, _se = topo.addr(h)
            g.remote_dma(out_ap=_view(T, r, name), in_ap=_view(T, r, name), remote_sem=T.sem["f_%s" % name],
                         local_sem=T.sem.sent, pid=pid, routing_id=rid, dma_engine_mask=m)
            sent += len(_bits(m))
        else:
            trs = []
            for name in step:
                h, m = feeds[name]
                rid, pid, _se = topo.addr(h)
                trs.append(RemoteDMATransfer(dst_ids=[DstId(rid=rid, pnc=pid)], dma_engine_mask=m,
                                             remote_sem=T.sem["f_%s" % name], src=_view(T, r, name),
                                             dst=_view(T, r, name)))
                sent += len(_bits(m))
            g.remote_dma_fused(trs, local_sem=T.sem.sent)
    g.wait_ge(T.sem.sent, sent)
    hs_of = [_helpers(T, topo, s) for s in range(N)]
    got = set()

    def need(s, lo, hi):
        if s == r:
            for i in _chunks_of(lo, hi):
                if ("q", i) not in got:
                    got.add(("q", i))
                    g.tensor.wait_ge(T.sem["qz%d" % i], 1)
            return
        for name, (_k, plo, phi, car) in PIECES.items():
            if plo < hi and phi > lo and (s, name) not in got:
                got.add((s, name))
                sender = T.cores[s] if car < 0 else hs_of[s][car]
                g.tensor.wait_ge(T.sem["a%d_%s" % (s, name)], len(_bits(_fan_mask(T, topo, sender, s))))

    seq = [((r - d) % N, q) for d in range(N) for q in WAVES]
    done = [0] * NQ
    for j, q in seq:
        k = (r - j) % N
        a = CW + q * CH
        need(k, 0, CW)
        need(j, a, a + CH)
        done[q] += 1
        mm = g.tensor.matmul_mx(T.acc[:, 512 * q:512 * q + CH], T["Q%d" % k][:, 0:CW], T["S%d" % k][:, 0:CW],
                                T["Q%d" % j][:, a:a + CH], T["S%d" % j][:, a:a + CH], done[q] == 1, done[q] == N)
        if done[q] == N:
            mm.then_inc(T.sem["mm%d" % q], 1)
    mine = {"scalar": [], "sync": []}
    for n, q in enumerate(WAVES):
        ysb, bank, yo = T.yb[:, q * CH:(q + 1) * CH], T.acc[:, 512 * q:512 * q + CH], T.y[:, q * CH:(q + 1) * CH]
        if (len(WAVES) - 1 - n) % 2:
            g.scalar.wait_ge(T.sem["mm%d" % q], 1)
            g.scalar.activation(ysb, bank, ActivationFunctionType.Copy).then_inc(T.sem["cp%d" % q], 1)
            g.scalar.wait_ge(T.sem["cp%d" % q], 1)
            g.scalar.dma_start(yo, ysb).then_inc(T.sem["st%d" % q], 16)
            mine["scalar"].append(q)
        else:
            g.vector.wait_ge(T.sem["mm%d" % q], 1)
            g.vector.tensor_copy(ysb, bank).then_inc(T.sem["cp%d" % q], 1)
            g.sync.wait_ge(T.sem["cp%d" % q], 1)
            g.sync.dma_start(yo, ysb).then_inc(T.sem["st%d" % q], 16)
            mine["sync"].append(q)
    for q in mine["scalar"]:
        g.scalar.wait_ge(T.sem["st%d" % q], 16)
    for q in mine["sync"]:
        g.sync.wait_ge(T.sem["st%d" % q], 16)


def rank_program(g, core, T, topo):
    rank = T.rank_of(core)
    if rank is not None:
        _rank(g, core, rank, T, topo)
        return
    for s in range(N):
        hs = _helpers(T, topo, s)
        if core in hs:
            _helper(g, core, s, hs.index(core), T, topo)
            return
